import numpy as np
CORES = [7,14,21,28,35,42,49,56,71,78,85,92,99,106,113,120]
N = 16
H = 1
PERIODIC = True
def setup_inputs(rng):
    return {"x": rng.standard_normal((N, 128, 128), dtype=np.float32)}
def reference(x):
    W = x.shape[2]
    y = np.zeros((N, 128, W + 2 * H), x.dtype)
    for r in range(N):
        y[r][:, H:H + W] = x[r]
        left, right = r - 1, r + 1
        if PERIODIC:
            left, right = left % N, right % N
        if 0 <= left < N:
            y[r][:, :H] = x[left][:, W - H:]
        if 0 <= right < N:
            y[r][:, W + H:] = x[right][:, :H]
    return {"y": y}

@@ -1,0 +1,76 @@
+from concourse.bass import DstId, RemoteDMATransfer
+
+W = 128
+
+SCRATCH = {
+    "ybuf": ("sbuf", [128, W + 2], "float32"),
+    "relay": ("sbuf", [128, 1], "float32"),
+}
+SEMAPHORES = ["loaded", "evt", "stored"]
+
+LEFT_HELPER = 7
+RIGHT_HELPER = 3
+
+
+def _direct(topo, cores, r):
+    n = len(cores)
+    return topo.may_write(cores[r], cores[(r - 1) % n]) and topo.may_write(cores[r], cores[(r + 1) % n])
+
+
+def _dst(topo, c):
+    rid, pid, _se = topo.addr(c)
+    return DstId(rid=rid, pnc=pid)
+
+
+def rank_program(g, core, T, topo):
+    cores = list(T.cores)
+    n = len(cores)
+    rank = T.rank_of(core)
+
+    if rank is None:
+        k = core % 8
+        if k not in (LEFT_HELPER, RIGHT_HELPER):
+            return
+        owners = [r for r in range(n) if topo.chip(cores[r]) == topo.chip(core)]
+        if not owners or _direct(topo, cores, owners[0]):
+            return
+        r = owners[0]
+        if k == LEFT_HELPER:
+            dst_core, out = cores[(r - 1) % n], T.ybuf[:, W + 1:W + 2]
+        else:
+            dst_core, out = cores[(r + 1) % n], T.ybuf[:, 0:1]
+        rid, pid, _se = topo.addr(dst_core)
+        g.wait_ge(T.sem.evt, 8)
+        g.remote_dma(out, T.relay[:, 0:1], T.sem.evt, T.sem.evt, pid, rid, 0x00FF)
+        g.wait_ge(T.sem.evt, 16)
+        return
+
+    left, right = (rank - 1) % n, (rank + 1) % n
+    first, last = T.ybuf[:, 1:2], T.ybuf[:, W:W + 1]
+
+    g.sync.dma_start(T.ybuf[:, 1:W + 1], T.x[:, :]).then_inc(T.sem.loaded, 16)
+    g.wait_ge(T.sem.loaded, 16)
+
+    if _direct(topo, cores, rank):
+        g.remote_dma_fused([
+            RemoteDMATransfer(dst_ids=[_dst(topo, cores[left])], dma_engine_mask=0x000F, remote_sem=T.sem.evt,
+                              src=first, dst=T.ybuf[:, W + 1:W + 2]),
+            RemoteDMATransfer(dst_ids=[_dst(topo, cores[right])], dma_engine_mask=0x00F0, remote_sem=T.sem.evt,
+                              src=last, dst=T.ybuf[:, 0:1]),
+        ], local_sem=T.sem.evt)
+        total = 8
+    else:
+        base = topo.chip(core) * 8
+        g.remote_dma_fused([
+            RemoteDMATransfer(dst_ids=[_dst(topo, base + LEFT_HELPER)], dma_engine_mask=0x00FF, remote_sem=T.sem.evt,
+                              src=first, dst=T.relay[:, 0:1]),
+            RemoteDMATransfer(dst_ids=[_dst(topo, base + RIGHT_HELPER)], dma_engine_mask=0xFF00, remote_sem=T.sem.evt,
+                              src=last, dst=T.relay[:, 0:1]),
+        ], local_sem=T.sem.evt)
+        total = 16
+    for nb in (left, right):
+        total += 4 if _direct(topo, cores, nb) else 8
+
+    g.sync.wait_ge(T.sem.evt, total)
+    g.sync.dma_start(T.y[:, :], T.ybuf[:, :]).then_inc(T.sem.stored, 16)
+    g.sync.wait_ge(T.sem.stored, 16)

@@ -8,13 +8,18 @@ SCRATCH = {
 }
 SEMAPHORES = ["loaded", "evt", "stored"]
 
-LEFT_HELPER = 7
-RIGHT_HELPER = 3
+PORT_CORE = {0: 7, 1: 3}
 
 
-def _direct(topo, cores, r):
+def _plan(topo, cores, r):
     n = len(cores)
-    return topo.may_write(cores[r], cores[(r - 1) % n]) and topo.may_write(cores[r], cores[(r + 1) % n])
+    me = cores[r]
+    nbs = [cores[(r - 1) % n], cores[(r + 1) % n]]
+    base = topo.chip(me) * 8
+    if all(topo.may_write(me, nb) for nb in nbs):
+        other = base + PORT_CORE[1 - topo.die(me)]
+        return [(nb, other if topo.mates(topo.chip(me), topo.chip(nb)) else me) for nb in nbs]
+    return [(nbs[0], base + PORT_CORE[0]), (nbs[1], base + PORT_CORE[1])]
 
 
 def _dst(topo, c):
@@ -26,51 +31,39 @@ def rank_program(g, core, T, topo):
     cores = list(T.cores)
     n = len(cores)
     rank = T.rank_of(core)
+    halo = [T.ybuf[:, W + 1:W + 2], T.ybuf[:, 0:1]]
 
     if rank is None:
-        k = core % 8
-        if k not in (LEFT_HELPER, RIGHT_HELPER):
-            return
-        owners = [r for r in range(n) if topo.chip(cores[r]) == topo.chip(core)]
-        if not owners or _direct(topo, cores, owners[0]):
-            return
-        r = owners[0]
-        if k == LEFT_HELPER:
-            dst_core, out = cores[(r - 1) % n], T.ybuf[:, W + 1:W + 2]
-        else:
-            dst_core, out = cores[(r + 1) % n], T.ybuf[:, 0:1]
-        rid, pid, _se = topo.addr(dst_core)
-        g.wait_ge(T.sem.evt, 8)
-        g.remote_dma(out, T.relay[:, 0:1], T.sem.evt, T.sem.evt, pid, rid, 0x00FF)
-        g.wait_ge(T.sem.evt, 16)
+        for r in range(n):
+            if topo.chip(cores[r]) != topo.chip(core):
+                continue
+            for side, (nb, via) in enumerate(_plan(topo, cores, r)):
+                if via != core:
+                    continue
+                rid, pid, _se = topo.addr(nb)
+                g.wait_ge(T.sem.evt, 8)
+                g.remote_dma(halo[side], T.relay[:, 0:1], T.sem.evt, T.sem.evt, pid, rid, 0x00FF)
+                g.wait_ge(T.sem.evt, 16)
         return
 
-    left, right = (rank - 1) % n, (rank + 1) % n
-    first, last = T.ybuf[:, 1:2], T.ybuf[:, W:W + 1]
+    edge = [T.ybuf[:, 1:2], T.ybuf[:, W:W + 1]]
 
     g.sync.dma_start(T.ybuf[:, 1:W + 1], T.x[:, :]).then_inc(T.sem.loaded, 16)
     g.wait_ge(T.sem.loaded, 16)
 
-    if _direct(topo, cores, rank):
-        g.remote_dma_fused([
-            RemoteDMATransfer(dst_ids=[_dst(topo, cores[left])], dma_engine_mask=0x000F, remote_sem=T.sem.evt,
-                              src=first, dst=T.ybuf[:, W + 1:W + 2]),
-            RemoteDMATransfer(dst_ids=[_dst(topo, cores[right])], dma_engine_mask=0x00F0, remote_sem=T.sem.evt,
-                              src=last, dst=T.ybuf[:, 0:1]),
-        ], local_sem=T.sem.evt)
-        total = 8
-    else:
-        base = topo.chip(core) * 8
-        g.remote_dma_fused([
-            RemoteDMATransfer(dst_ids=[_dst(topo, base + LEFT_HELPER)], dma_engine_mask=0x00FF, remote_sem=T.sem.evt,
-                              src=first, dst=T.relay[:, 0:1]),
-            RemoteDMATransfer(dst_ids=[_dst(topo, base + RIGHT_HELPER)], dma_engine_mask=0xFF00, remote_sem=T.sem.evt,
-                              src=last, dst=T.relay[:, 0:1]),
-        ], local_sem=T.sem.evt)
-        total = 16
-    for nb in (left, right):
-        total += 4 if _direct(topo, cores, nb) else 8
+    plan = _plan(topo, cores, rank)
+    transfers = []
+    low_taken = any(via == core for _nb, via in plan)
+    for side, (nb, via) in enumerate(plan):
+        if via == core:
+            transfers.append(RemoteDMATransfer(dst_ids=[_dst(topo, nb)], dma_engine_mask=0x00FF,
+                                               remote_sem=T.sem.evt, src=edge[side], dst=halo[side]))
+        else:
+            m = 0xFF00 if (low_taken or side == 1) else 0x00FF
+            transfers.append(RemoteDMATransfer(dst_ids=[_dst(topo, via)], dma_engine_mask=m,
+                                               remote_sem=T.sem.evt, src=edge[side], dst=T.relay[:, 0:1]))
+    g.remote_dma_fused(transfers, local_sem=T.sem.evt)
 
-    g.sync.wait_ge(T.sem.evt, total)
+    g.sync.wait_ge(T.sem.evt, 32)
     g.sync.dma_start(T.y[:, :], T.ybuf[:, :]).then_inc(T.sem.stored, 16)
     g.sync.wait_ge(T.sem.stored, 16)

from concourse.bass import DstId, RemoteDMATransfer

W = 128

SCRATCH = {
    "ybuf": ("sbuf", [128, W + 2], "float32"),
    "relay": ("sbuf", [128, 1], "float32"),
}
SEMAPHORES = ["loaded", "evt", "stored"]

PORT_CORE = {0: 7, 1: 3}


def _plan(topo, cores, r):
    n = len(cores)
    me = cores[r]
    nbs = [cores[(r - 1) % n], cores[(r + 1) % n]]
    base = topo.chip(me) * 8
    if all(topo.may_write(me, nb) for nb in nbs):
        other = base + PORT_CORE[1 - topo.die(me)]
        return [(nb, other if topo.mates(topo.chip(me), topo.chip(nb)) else me) for nb in nbs]
    return [(nbs[0], base + PORT_CORE[0]), (nbs[1], base + PORT_CORE[1])]


def _dst(topo, c):
    rid, pid, _se = topo.addr(c)
    return DstId(rid=rid, pnc=pid)


def rank_program(g, core, T, topo):
    cores = list(T.cores)
    n = len(cores)
    rank = T.rank_of(core)
    halo = [T.ybuf[:, W + 1:W + 2], T.ybuf[:, 0:1]]

    if rank is None:
        for r in range(n):
            if topo.chip(cores[r]) != topo.chip(core):
                continue
            for side, (nb, via) in enumerate(_plan(topo, cores, r)):
                if via != core:
                    continue
                rid, pid, _se = topo.addr(nb)
                g.wait_ge(T.sem.evt, 8)
                g.remote_dma(halo[side], T.relay[:, 0:1], T.sem.evt, T.sem.evt, pid, rid, 0x00FF)
                g.wait_ge(T.sem.evt, 16)
        return

    edge = [T.ybuf[:, 1:2], T.ybuf[:, W:W + 1]]

    g.sync.dma_start(T.ybuf[:, 1:W + 1], T.x[:, :]).then_inc(T.sem.loaded, 16)
    g.wait_ge(T.sem.loaded, 16)

    plan = _plan(topo, cores, rank)
    transfers = []
    low_taken = any(via == core for _nb, via in plan)
    for side, (nb, via) in enumerate(plan):
        if via == core:
            transfers.append(RemoteDMATransfer(dst_ids=[_dst(topo, nb)], dma_engine_mask=0x00FF,
                                               remote_sem=T.sem.evt, src=edge[side], dst=halo[side]))
        else:
            m = 0xFF00 if (low_taken or side == 1) else 0x00FF
            transfers.append(RemoteDMATransfer(dst_ids=[_dst(topo, via)], dma_engine_mask=m,
                                               remote_sem=T.sem.evt, src=edge[side], dst=T.relay[:, 0:1]))
    g.remote_dma_fused(transfers, local_sem=T.sem.evt)

    g.sync.wait_ge(T.sem.evt, 32)
    g.sync.dma_start(T.y[:, :], T.ybuf[:, :]).then_inc(T.sem.stored, 16)
    g.sync.wait_ge(T.sem.stored, 16)
